import numpy as np
import ml_dtypes


def mxq(x, axis, fmt="e4m3"):
    dtype, down = {"e4m3": (ml_dtypes.float8_e4m3fn, 7), "e5m2": (ml_dtypes.float8_e5m2, 14)}[fmt]
    v = np.moveaxis(np.asarray(x, np.float32).astype(ml_dtypes.bfloat16).astype(np.float64), axis, -1)
    blocks = v.reshape(v.shape[:-1] + (-1, 32))
    amax = np.abs(blocks).max(-1, keepdims=True)
    byte = np.maximum(np.where(amax > 0, np.frexp(amax)[1] - 1 + 127, 0) - down, 1)
    scale = np.exp2(byte - 127.0)
    codes = (blocks / scale).astype(np.float32).astype(dtype).astype(np.float64)
    return np.moveaxis((codes * scale).reshape(v.shape), -1, axis)


WIDE = False


def mx_kscale(k):
    if not WIDE:
        return np.ones(k)
    levels = np.array([10, -10, 5, -5, 0])
    if k % 512:
        return np.exp2(np.random.permutation(np.resize(levels, k // 32))).repeat(32)
    a = np.empty((k // 512, 16))
    for p in range(k // 512):
        a[p, :8] = np.random.permutation(np.resize(levels, 8))
        for g in range(8):
            far = levels[np.abs(levels - a[p, g]) >= 10]
            a[p, g + 8] = far[np.random.randint(len(far))]
    return np.exp2(a.ravel()).repeat(32)


def f64(x):
    return np.asarray(x).astype(np.float64)


def striped(idx):
    return np.tile(idx.reshape(-1, 16).T, (8, 1)).astype(np.uint16)


def unstriped(offs):
    return offs[:16].T.reshape(-1).astype(np.int64)


E2M1 = np.array([0.0, 0.5, 1.0, 1.5, 2.0, 3.0, 4.0, 6.0, -0.0, -0.5, -1.0, -1.5, -2.0, -3.0, -4.0, -6.0])


def pack_weight(w, fmt):
    k, n = w.shape
    w = f64(np.asarray(w, np.float32).astype(ml_dtypes.bfloat16)).reshape(k // 32, 32, n)
    amax = np.abs(w).max(1)
    if fmt == "e4m3":
        byte = np.frexp(amax)[1] - 1 + 127 - 7
    else:
        mant, ex = np.frexp(amax / 6.0)
        byte = np.where(mant > 0.5, ex, ex - 1) + 127
    byte = np.clip(np.where(amax > 0, byte, 1), 1, 254)
    scaled = (w * np.exp2(127.0 - byte)[:, None, :]).reshape(k, n).astype(np.float32)
    by_word = np.ascontiguousarray(scaled.reshape(k // 512, 128, 4, n).transpose(0, 1, 3, 2))
    if fmt == "e4m3":
        words = by_word.astype(ml_dtypes.float8_e4m3fn).view(np.uint8)
    else:
        c = by_word.astype(ml_dtypes.float4_e2m1fn).view(np.uint8) & 0xF
        words = (c[..., 0::2] | (c[..., 1::2] << 4)).reshape(k // 512, 128, 2 * n)
    return np.ascontiguousarray(words), np.ascontiguousarray(byte.astype(np.uint8).reshape(k // 512, 16, n))


def unpack_weight(words, scales, fmt):
    g, _, n = scales.shape
    words = np.ascontiguousarray(words).reshape(g, 128, n, -1)
    if fmt == "e4m3":
        vals = words.view(ml_dtypes.float8_e4m3fn).astype(np.float64)
    else:
        nib = np.empty((g, 128, n, 4), np.uint8)
        nib[..., 0::2] = words & 0xF
        nib[..., 1::2] = words >> 4
        vals = E2M1[nib]
    vals = vals * np.repeat(np.exp2(scales.astype(np.float64) - 127.0), 8, axis=1)[..., None]
    return vals.transpose(0, 1, 3, 2).reshape(g * 512, n)


def gelu(v):
    return 0.5 * v * (1.0 + np.tanh(np.sqrt(2.0 / np.pi) * (v + 0.044715 * v**3)))


K, T, S, T2, P, H, M, N = 1536, 2048, 1024, 2048, 1024, 512, 1024, 384

def setup_inputs():
    n = np.random.standard_normal
    s, u, u2 = mx_kscale(K)[:, None], mx_kscale(H)[:, None], mx_kscale(M)[:, None]
    tab_words, tab_scales = pack_weight(n((K, T)) * s, "e4m3")
    wm_words, wm_scales = pack_weight(n((H, M)) / np.sqrt(H) / u, "e2m1")
    return {
        "tab_words": tab_words, "tab_scales": tab_scales,
        "offs": striped(np.random.permutation(T)[:S]),
        "w1": (1.4 * n((K, H)) / np.sqrt(K) / s).astype(np.float32),
        "b1": (0.5 * n(H)).astype(np.float32),
        "gain": (np.exp(0.3 * n(H)) * u[:, 0]).astype(np.float32),
        "page0": (n((H, T2)) * u).astype(np.float32),
        "wgs": np.exp(0.3 * n((128, S))).astype(np.float32),
        "offs2": striped(np.random.permutation(T2)[:S]),
        "offs3": striped(np.random.permutation(T2)[:P]),
        "offs4": striped(np.random.permutation(T2)[:P]),
        "wm_words": wm_words, "wm_scales": wm_scales,
        "gain2": (np.exp(0.3 * n(M)) * u2[:, 0]).astype(np.float32),
        "wd": (n((H, N)) / np.sqrt(H) / u).astype(np.float32),
        "wt": (1.5 * n((M, N)) / np.sqrt(M) / u2).astype(np.float32),
    }

def reference(tab_words, tab_scales, offs, w1, b1, gain, page0, wgs, offs2, offs3, offs4,
              wm_words, wm_scales, gain2, wd, wt):
    v = unpack_weight(tab_words, tab_scales, "e4m3")[:, unstriped(offs)]
    h = f64(gain)[:, None] * np.tanh((mxq(f64(w1), 0, "e4m3").T @ v) + f64(b1)[:, None])
    before = f64(page0)
    page = before.copy()
    page[:, unstriped(offs2)] = np.tile(f64(wgs), (H // 128, 1)) * h
    x = page[:, unstriped(offs3)] - before[:, unstriped(offs4)]
    xq = mxq(x, 0, "e4m3")
    wm = unpack_weight(wm_words, wm_scales, "e2m1")
    d = f64(gain2)[:, None] * np.tanh(wm.T @ xq)
    return mxq(f64(wd), 0, "e4m3").T @ xq + mxq(f64(wt), 0, "e4m3").T @ mxq(d, 0, "e4m3")

@@ -1,0 +1,240 @@
+from contextlib import ExitStack
+
+import concourse.mybir as mybir
+
+K, T, S, T2, PJ, H, M, N = 1536, 2048, 1024, 2048, 1024, 512, 1024, 384
+FLOPS = 2 * (K * H * S + H * M * PJ + H * N * PJ + M * N * PJ)
+
+F32 = mybir.dt.float32
+BF16 = mybir.dt.bfloat16
+I32 = mybir.dt.int32
+U32 = mybir.dt.uint32
+U16 = mybir.dt.uint16
+U8 = mybir.dt.uint8
+FP8X4 = mybir.dt.float8_e4m3fn_x4
+FP4X4 = mybir.dt.float4_e2m1fn_x4
+TANH = mybir.ActivationFunctionType.Tanh
+COPY = mybir.ActivationFunctionType.Copy
+MULT = mybir.AluOpType.mult
+SUB = mybir.AluOpType.subtract
+
+P = 128
+PACK = 4
+KP = P * PACK
+BANK = 512
+CH = 256
+SUBC = 128
+
+
+def tile_list_sleeper_crack_scores_kernel(
+    tc, tab_words, tab_scales, offs, w1, b1, gain, page0, wgs, offs2, offs3, offs4,
+    wm_words, wm_scales, gain2, wd, wt, out,
+):
+    nc = tc.nc
+    ka = K // KP
+    mb = M // KP
+
+    with ExitStack() as ctx:
+        keep = ctx.enter_context(tc.tile_pool(name="keep", bufs=1))
+        ring = ctx.enter_context(tc.tile_pool(name="ring", bufs=2))
+        psum = ctx.enter_context(tc.psum_pool(name="psum", bufs=1))
+
+        def load_list(src, name):
+            tile = keep.tile([P, src.shape[1]], U16, name=name)
+            nc.sync.dma_start(tile[:], src)
+            return tile
+
+        def load_rows(rows, name):
+            raw = ring.tile([P, PACK, rows.shape[1]], F32, name=name, tag="raw", bufs=3)
+            nc.sync.dma_start(out=raw[:], in_=rows.rearrange("(p j) w -> p j w", j=PACK))
+            return raw
+
+        def quantise(grouped, width, name, pool, tag, bufs):
+            codes = pool.tile([P, width], U32, name=name + "_codes", tag=tag + "c", bufs=bufs, align_bytes=64)
+            plane = pool.tile([P, width], U8, name=name + "_plane", tag=tag + "p", bufs=bufs, align_bytes=64)
+            nc.vector.quantize_mx(out=codes[:].bitcast(FP8X4), scales=plane[:], in_=grouped)
+            return codes, plane
+
+        tab_plane = keep.tile([P, T], U8, name="tab_plane", align_bytes=64)
+        nc.gpsimd.memset(tab_plane[:].bitcast(I32), 0)
+        for q in range(4):
+            nc.gpsimd.dma_start(
+                out=tab_plane[32 * q : 32 * q + 4 * ka, :].bitcast(I32),
+                in_=tab_scales[:, 4 * q : 4 * q + 4, :].bitcast(I32),
+            )
+        b1_sb = keep.tile([P, PACK], F32, name="b1_sb")
+        nc.gpsimd.dma_start(out=b1_sb[:], in_=b1.rearrange("(p t) -> p t", t=PACK))
+        gain_sb = keep.tile([P, PACK], F32, name="gain_sb")
+        nc.gpsimd.dma_start(out=gain_sb[:], in_=gain.rearrange("(p t) -> p t", t=PACK))
+        wm_plane_raw = keep.tile([P, M], U8, name="wm_plane_raw", align_bytes=64)
+        nc.gpsimd.memset(wm_plane_raw[:].bitcast(I32), 0)
+        for q in range(4):
+            nc.gpsimd.dma_start(
+                out=wm_plane_raw[32 * q : 32 * q + 4, :].bitcast(I32),
+                in_=wm_scales[0, 4 * q : 4 * q + 4, :].bitcast(I32),
+            )
+        gain2_sb = keep.tile([P, mb, PACK], F32, name="gain2_sb")
+        nc.gpsimd.dma_start(out=gain2_sb[:], in_=gain2.rearrange("(b p t) -> p b t", p=P, t=PACK))
+
+        list1 = load_list(offs, "list1")
+        wm_raw = keep.tile([P, 2 * M], U8, name="wm_raw", align_bytes=64)
+        picked = []
+        w1q = []
+        for a in range(ka):
+            words = keep.tile([P, T], I32, name="tab%d" % a, align_bytes=64)
+            nc.sync.dma_start(out=words[:], in_=tab_words[a].rearrange("p t i -> p (t i)").bitcast(I32))
+            if a == 0:
+                nc.sync.dma_start(out=wm_raw[:].bitcast(I32), in_=wm_words[0].bitcast(I32))
+            raw = load_rows(w1[a * KP : (a + 1) * KP, :], "w1raw%d" % a)
+            got = keep.tile([P, S], U32, name="picked%d" % a, align_bytes=64)
+            nc.vector.tensor_copy(got[:], words[:].bitcast(U32).indirect(list1[:]))
+            picked.append(got)
+            if a == 0:
+                picked_plane = keep.tile([P, S], U8, name="picked_plane", align_bytes=64)
+                nc.vector.tensor_copy(picked_plane[:], tab_plane[:].indirect(list1[:]))
+            grouped = ring.tile([P, PACK, P, PACK], BF16, name="w1g%d" % a, tag="grouped", bufs=2, align_bytes=64)
+            nc.scalar.copy(
+                out=grouped[:].rearrange("p t m j -> p m j t"),
+                in_=raw[:].rearrange("p j (m t) -> p m j t", t=PACK),
+            )
+            w1q.append(quantise(grouped[:].rearrange("p t m j -> p (t m j)"), H, "w1q%d" % a, keep, "w1q%d" % a, 1))
+
+        wm_codes = keep.tile([P, 2 * M], U8, name="wm_codes", align_bytes=64)
+        nc.vector.tensor_copy(
+            out=wm_codes[:].bitcast(U16).rearrange("p (b t q) -> p b t q", b=mb, t=PACK),
+            in_=wm_raw[:].bitcast(U16).rearrange("p (b q t) -> p b t q", b=mb, t=PACK),
+        )
+        wm_plane = keep.tile([P, M], U8, name="wm_plane", align_bytes=64)
+        nc.vector.tensor_copy(
+            out=wm_plane[:].rearrange("p (b t q) -> p b t q", b=mb, t=PACK),
+            in_=wm_plane_raw[:].rearrange("p (b q t) -> p b t q", b=mb, t=PACK),
+        )
+
+        page_rows = page0.rearrange("(p t) c -> p t c", t=PACK)
+        wgs_rows = wgs.rearrange("(q t) j -> q t j", t=PACK)
+        list4 = load_list(offs4, "list4")
+        pages = [keep.tile([P, T2], F32, name="page%d" % t) for t in range(PACK)]
+        wg_first = keep.tile([P, 1, S], F32, name="wg_first")
+        wg_rest = keep.tile([P, PACK - 1, S], F32, name="wg_rest")
+        nc.sync.dma_start(out=pages[0][:], in_=page_rows[:, 0, :])
+        list2 = load_list(offs2, "list2")
+        for q in range(4):
+            nc.sync.dma_start(out=wg_first[32 * q : 32 * q + 32], in_=wgs_rows[:, 0:1, :])
+        nc.sync.dma_start(out=pages[1][:], in_=page_rows[:, 1, :])
+        for q in range(4):
+            nc.sync.dma_start(out=wg_rest[32 * q : 32 * q + 32], in_=wgs_rows[:, 1:PACK, :])
+        for t in range(2, PACK):
+            nc.sync.dma_start(out=pages[t][:], in_=page_rows[:, t, :])
+        list3 = load_list(offs3, "list3")
+        wd_raw = load_rows(wd, "wdraw")
+        wt_raw = [load_rows(wt[b * KP : (b + 1) * KP, :], "wtraw%d" % b) for b in range(mb)]
+        wg = [wg_first[:, 0, :]] + [wg_rest[:, t, :] for t in range(PACK - 1)]
+
+        halves = S // BANK
+
+        def stage1_pass(acc, t, half, a):
+            codes, plane = w1q[a]
+            cols = slice(half * BANK, (half + 1) * BANK)
+            nc.tensor.matmul_mx(
+                out=acc[:],
+                lhsT=codes[:, t * P : (t + 1) * P].bitcast(FP8X4),
+                lhsT_scale=plane[:, t * P : (t + 1) * P],
+                rhs=picked[a][:, cols].bitcast(FP8X4),
+                rhs_scale=picked_plane[4 * a : P, cols],
+                start=(a == 0),
+                stop=(a == ka - 1),
+            )
+
+        accs = {}
+        for t in range(2):
+            for half in range(halves):
+                accs[(t, half)] = psum.tile([P, BANK], F32, name="h_acc%d%d" % (t, half), tag="z", bufs=4)
+        for a in range(ka):
+            for t in range(2):
+                for half in range(halves):
+                    stage1_pass(accs[(t, half)], t, half, a)
+
+        before = []
+        for t in range(PACK):
+            old = keep.tile([P, PJ], F32, name="before%d" % t)
+            nc.vector.tensor_copy(old[:], pages[t][:].indirect(list4[:]))
+            before.append(old)
+            nc.scalar.activation(out=wg[t], in_=wg[t], func=COPY, scale=gain_sb[:, t : t + 1])
+            feat = ring.tile([P, S], F32, name="feat%d" % t, tag="feat_or_diff")
+            for half in range(halves):
+                if t >= 2:
+                    accs[(t, half)] = psum.tile([P, BANK], F32, name="h_acc%d%d" % (t, half), tag="z", bufs=4)
+                    for a in range(ka):
+                        stage1_pass(accs[(t, half)], t, half, a)
+                nc.scalar.activation(
+                    out=feat[:, half * BANK : (half + 1) * BANK], in_=accs[(t, half)][:],
+                    func=TANH, bias=b1_sb[:, t : t + 1],
+                )
+            nc.vector.tensor_tensor(pages[t][:].indirect(list2[:]), feat[:], wg[t], MULT)
+
+        def interleave(grouped, raw):
+            nc.scalar.copy(
+                out=grouped.rearrange("p (c i) t -> p c t i", i=4),
+                in_=raw.rearrange("p t (c i) -> p c t i", i=4),
+            )
+
+        outw = []
+        for name, raw in (("wd", wd_raw), ("wt0", wt_raw[0]), ("wt1", wt_raw[1])):
+            grouped = ring.tile([P, N, PACK], BF16, name=name + "g", tag="grouped", bufs=2, align_bytes=64)
+            interleave(grouped[:], raw[:])
+            outw.append(quantise(grouped[:].rearrange("p n j -> p (n j)"), N, name, keep, name, 1))
+
+        out_rows = out.rearrange("(i p) j -> p i j", p=P)
+        for c in range(PJ // CH):
+            cols = slice(c * CH, (c + 1) * CH)
+            diff = ring.tile([P, PACK, CH], F32, name="diff%d" % c, tag="feat_or_diff")
+            for t in range(PACK):
+                nc.vector.tensor_tensor(
+                    diff[:, t, :], pages[t][:].indirect(list3[:, c * CH // 16 : (c + 1) * CH // 16]),
+                    before[t][:, cols], SUB,
+                )
+            xg = ring.tile([P, CH, PACK], BF16, name="xg%d" % c, tag="xg", align_bytes=64)
+            interleave(xg[:], diff[:])
+            x_codes, x_plane = quantise(xg[:].rearrange("p c t -> p (c t)"), CH, "x%d" % c, ring, "x", 4)
+
+            moving = [(x_codes, x_plane)]
+            for b in range(mb):
+                bent = ring.tile([P, CH, PACK], F32, name="bent%d_%d" % (c, b), tag="bent", bufs=4)
+                for s in range(CH // SUBC):
+                    sub = slice(s * SUBC, (s + 1) * SUBC)
+                    z = psum.tile([P, PACK, SUBC], F32, name="z%d_%d_%d" % (c, b, s), tag="z", bufs=4)
+                    for t in range(PACK):
+                        m0 = (b * PACK + t) * P
+                        nc.tensor.matmul_mx(
+                            out=z[:, t, :],
+                            lhsT=wm_codes[:, 2 * m0 : 2 * (m0 + P)].bitcast(FP4X4),
+                            lhsT_scale=wm_plane[:, m0 : m0 + P],
+                            rhs=x_codes[:, sub].bitcast(FP8X4),
+                            rhs_scale=x_plane[:, sub],
+                            start=True,
+                            stop=True,
+                        )
+                    nc.scalar.activation(out=bent[:, sub, :], in_=z[:].rearrange("p t j -> p j t"), func=TANH)
+                dg = ring.tile([P, CH, PACK], BF16, name="dg%d_%d" % (c, b), tag="dg", bufs=3, align_bytes=64)
+                nc.vector.tensor_tensor(
+                    dg[:], bent[:], gain2_sb[:, b : b + 1, :].to_broadcast([P, CH, PACK]), MULT
+                )
+                moving.append(quantise(dg[:].rearrange("p c t -> p (c t)"), CH, "d%d_%d" % (c, b), ring, "d", 4))
+
+            staged = ring.tile([P, N // P, CH], F32, name="staged%d" % c, tag="staged")
+            for first, count in ((0, 2), (2, 1)):
+                acc = psum.tile([P, count, CH], F32, name="o%d_%d" % (c, first), tag="o", bufs=4)
+                for i in range(count):
+                    ncols = slice((first + i) * P, (first + i + 1) * P)
+                    for g in range(len(moving)):
+                        nc.tensor.matmul_mx(
+                            out=acc[:, i, :],
+                            lhsT=outw[g][0][:, ncols].bitcast(FP8X4),
+                            lhsT_scale=outw[g][1][:, ncols],
+                            rhs=moving[g][0][:].bitcast(FP8X4),
+                            rhs_scale=moving[g][1][:],
+                            start=(g == 0),
+                            stop=(g == len(moving) - 1),
+                        )
+                nc.scalar.copy(out=staged[:, first : first + count, :], in_=acc[:])
+            nc.sync.dma_start(out=out_rows[:, :, cols], in_=staged[:])

@@ -22,7 +22,7 @@ P = 128
 PACK = 4
 KP = P * PACK
 BANK = 512
-CH = 256
+CHUNKS = (256, 256, 256, 128, 128)
 SUBC = 128
 
 
@@ -62,30 +62,28 @@ def tile_list_sleeper_crack_scores_kernel(
                 out=tab_plane[32 * q : 32 * q + 4 * ka, :].bitcast(I32),
                 in_=tab_scales[:, 4 * q : 4 * q + 4, :].bitcast(I32),
             )
-        b1_sb = keep.tile([P, PACK], F32, name="b1_sb")
-        nc.gpsimd.dma_start(out=b1_sb[:], in_=b1.rearrange("(p t) -> p t", t=PACK))
-        gain_sb = keep.tile([P, PACK], F32, name="gain_sb")
-        nc.gpsimd.dma_start(out=gain_sb[:], in_=gain.rearrange("(p t) -> p t", t=PACK))
         wm_plane_raw = keep.tile([P, M], U8, name="wm_plane_raw", align_bytes=64)
-        nc.gpsimd.memset(wm_plane_raw[:].bitcast(I32), 0)
-        for q in range(4):
-            nc.gpsimd.dma_start(
-                out=wm_plane_raw[32 * q : 32 * q + 4, :].bitcast(I32),
-                in_=wm_scales[0, 4 * q : 4 * q + 4, :].bitcast(I32),
-            )
-        gain2_sb = keep.tile([P, mb, PACK], F32, name="gain2_sb")
-        nc.gpsimd.dma_start(out=gain2_sb[:], in_=gain2.rearrange("(b p t) -> p b t", p=P, t=PACK))
+        nc.vector.memset(wm_plane_raw[:].bitcast(I32), 0)
 
         list1 = load_list(offs, "list1")
         wm_raw = keep.tile([P, 2 * M], U8, name="wm_raw", align_bytes=64)
         picked = []
         w1q = []
+        b1_sb = keep.tile([P, PACK], F32, name="b1_sb")
+        gain_sb = keep.tile([P, PACK], F32, name="gain_sb")
+
+        gain2_sb = keep.tile([P, mb, PACK], F32, name="gain2_sb")
+        nc.scalar.dma_start(out=b1_sb[:], in_=b1.rearrange("(p t) -> p t", t=PACK))
+        nc.scalar.dma_start(out=gain_sb[:], in_=gain.rearrange("(p t) -> p t", t=PACK))
+        nc.scalar.dma_start(out=gain2_sb[:], in_=gain2.rearrange("(b p t) -> p b t", p=P, t=PACK))
+
         for a in range(ka):
             words = keep.tile([P, T], I32, name="tab%d" % a, align_bytes=64)
             nc.sync.dma_start(out=words[:], in_=tab_words[a].rearrange("p t i -> p (t i)").bitcast(I32))
+            raw = load_rows(w1[a * KP : (a + 1) * KP, :], "w1raw%d" % a)
             if a == 0:
                 nc.sync.dma_start(out=wm_raw[:].bitcast(I32), in_=wm_words[0].bitcast(I32))
-            raw = load_rows(w1[a * KP : (a + 1) * KP, :], "w1raw%d" % a)
+                nc.sync.dma_start(out=wm_plane_raw[0:16, :].bitcast(I32), in_=wm_scales[0].bitcast(I32))
             got = keep.tile([P, S], U32, name="picked%d" % a, align_bytes=64)
             nc.vector.tensor_copy(got[:], words[:].bitcast(U32).indirect(list1[:]))
             picked.append(got)
@@ -93,7 +91,8 @@ def tile_list_sleeper_crack_scores_kernel(
                 picked_plane = keep.tile([P, S], U8, name="picked_plane", align_bytes=64)
                 nc.vector.tensor_copy(picked_plane[:], tab_plane[:].indirect(list1[:]))
             grouped = ring.tile([P, PACK, P, PACK], BF16, name="w1g%d" % a, tag="grouped", bufs=2, align_bytes=64)
-            nc.scalar.copy(
+            copy = nc.vector.tensor_copy if a == ka - 1 else nc.scalar.copy
+            copy(
                 out=grouped[:].rearrange("p t m j -> p m j t"),
                 in_=raw[:].rearrange("p j (m t) -> p m j t", t=PACK),
             )
@@ -109,26 +108,33 @@ def tile_list_sleeper_crack_scores_kernel(
             out=wm_plane[:].rearrange("p (b t q) -> p b t q", b=mb, t=PACK),
             in_=wm_plane_raw[:].rearrange("p (b q t) -> p b t q", b=mb, t=PACK),
         )
+        for q in range(1, 4):
+            nc.gpsimd.dma_start(
+                out=wm_plane[32 * q : 32 * q + 4, :].bitcast(I32), in_=wm_plane[4 * q : 4 * q + 4, :].bitcast(I32)
+            )
 
         page_rows = page0.rearrange("(p t) c -> p t c", t=PACK)
         wgs_rows = wgs.rearrange("(q t) j -> q t j", t=PACK)
         list4 = load_list(offs4, "list4")
         pages = [keep.tile([P, T2], F32, name="page%d" % t) for t in range(PACK)]
-        wg_first = keep.tile([P, 1, S], F32, name="wg_first")
-        wg_rest = keep.tile([P, PACK - 1, S], F32, name="wg_rest")
+        wg = [keep.tile([P, S], F32, name="wg%d" % t) for t in range(PACK)]
+
+        def load_wgs(t, cols):
+            for q in (0, 2, 1, 3):
+                nc.sync.dma_start(out=wg[t][32 * q : 32 * q + 32, cols], in_=wgs_rows[:, t, cols])
+
         nc.sync.dma_start(out=pages[0][:], in_=page_rows[:, 0, :])
+        load_wgs(0, slice(0, BANK))
         list2 = load_list(offs2, "list2")
-        for q in range(4):
-            nc.sync.dma_start(out=wg_first[32 * q : 32 * q + 32], in_=wgs_rows[:, 0:1, :])
-        nc.sync.dma_start(out=pages[1][:], in_=page_rows[:, 1, :])
-        for q in range(4):
-            nc.sync.dma_start(out=wg_rest[32 * q : 32 * q + 32], in_=wgs_rows[:, 1:PACK, :])
-        for t in range(2, PACK):
+        load_wgs(0, slice(BANK, S))
+        for t in range(1, PACK):
             nc.sync.dma_start(out=pages[t][:], in_=page_rows[:, t, :])
-        list3 = load_list(offs3, "list3")
-        wd_raw = load_rows(wd, "wdraw")
-        wt_raw = [load_rows(wt[b * KP : (b + 1) * KP, :], "wtraw%d" % b) for b in range(mb)]
-        wg = [wg_first[:, 0, :]] + [wg_rest[:, t, :] for t in range(PACK - 1)]
+            load_wgs(t, slice(0, S))
+            if t == 1:
+                list3 = load_list(offs3, "list3")
+                wd_raw = load_rows(wd, "wdraw")
+            if t == 2:
+                wt_raw = [load_rows(wt[b * KP : (b + 1) * KP, :], "wtraw%d" % b) for b in range(mb)]
 
         halves = S // BANK
 
@@ -159,18 +165,29 @@ def tile_list_sleeper_crack_scores_kernel(
             old = keep.tile([P, PJ], F32, name="before%d" % t)
             nc.vector.tensor_copy(old[:], pages[t][:].indirect(list4[:]))
             before.append(old)
-            nc.scalar.activation(out=wg[t], in_=wg[t], func=COPY, scale=gain_sb[:, t : t + 1])
             feat = ring.tile([P, S], F32, name="feat%d" % t, tag="feat_or_diff")
             for half in range(halves):
+                cols = slice(half * BANK, (half + 1) * BANK)
+                nc.scalar.activation(out=wg[t][:, cols], in_=wg[t][:, cols], func=COPY, scale=gain_sb[:, t : t + 1])
                 if t >= 2:
                     accs[(t, half)] = psum.tile([P, BANK], F32, name="h_acc%d%d" % (t, half), tag="z", bufs=4)
                     for a in range(ka):
                         stage1_pass(accs[(t, half)], t, half, a)
                 nc.scalar.activation(
-                    out=feat[:, half * BANK : (half + 1) * BANK], in_=accs[(t, half)][:],
-                    func=TANH, bias=b1_sb[:, t : t + 1],
+                    out=feat[:, cols], in_=accs[(t, half)][:], func=TANH, bias=b1_sb[:, t : t + 1]
                 )
-            nc.vector.tensor_tensor(pages[t][:].indirect(list2[:]), feat[:], wg[t], MULT)
+            pieces = halves if t == 0 else 1
+            for piece in range(pieces):
+                lo, hi = piece * S // pieces, (piece + 1) * S // pieces
+                nc.vector.tensor_tensor(
+                    pages[t][:].indirect(list2[:, lo // 16 : hi // 16]), feat[:, lo:hi], wg[t][:, lo:hi], MULT
+                )
+
+        gain2_rows = keep.tile([P, mb, max(CHUNKS), PACK], F32, name="gain2_rows")
+        for b in range(mb):
+            nc.scalar.copy(
+                out=gain2_rows[:, b], in_=gain2_sb[:, b : b + 1, :].to_broadcast([P, max(CHUNKS), PACK])
+            )
 
         def interleave(grouped, raw):
             nc.scalar.copy(
@@ -185,22 +202,31 @@ def tile_list_sleeper_crack_scores_kernel(
             outw.append(quantise(grouped[:].rearrange("p n j -> p (n j)"), N, name, keep, name, 1))
 
         out_rows = out.rearrange("(i p) j -> p i j", p=P)
-        for c in range(PJ // CH):
-            cols = slice(c * CH, (c + 1) * CH)
-            diff = ring.tile([P, PACK, CH], F32, name="diff%d" % c, tag="feat_or_diff")
+        starts = [sum(CHUNKS[:c]) for c in range(len(CHUNKS))]
+        xq = {}
+        bent = {}
+        sums = {}
+
+        def differences(c):
+            width = CHUNKS[c]
+            cols = slice(starts[c], starts[c] + width)
+            diff = ring.tile([P, PACK, width], F32, name="diff%d" % c, tag="feat_or_diff")
             for t in range(PACK):
                 nc.vector.tensor_tensor(
-                    diff[:, t, :], pages[t][:].indirect(list3[:, c * CH // 16 : (c + 1) * CH // 16]),
+                    diff[:, t, :], pages[t][:].indirect(list3[:, cols.start // 16 : cols.stop // 16]),
                     before[t][:, cols], SUB,
                 )
-            xg = ring.tile([P, CH, PACK], BF16, name="xg%d" % c, tag="xg", align_bytes=64)
+            xg = ring.tile([P, width, PACK], BF16, name="xg%d" % c, tag="xg", align_bytes=64)
             interleave(xg[:], diff[:])
-            x_codes, x_plane = quantise(xg[:].rearrange("p c t -> p (c t)"), CH, "x%d" % c, ring, "x", 4)
+            xq[c] = quantise(xg[:].rearrange("p c t -> p (c t)"), width, "x%d" % c, ring, "x", len(CHUNKS))
 
-            moving = [(x_codes, x_plane)]
+        def bend(c):
+            width = CHUNKS[c]
+            x_codes, x_plane = xq[c]
             for b in range(mb):
-                bent = ring.tile([P, CH, PACK], F32, name="bent%d_%d" % (c, b), tag="bent", bufs=4)
-                for s in range(CH // SUBC):
+                tile = ring.tile([P, width, PACK], F32, name="bent%d_%d" % (c, b), tag="bent", bufs=6)
+                bent[(c, b)] = tile
+                for s in range(width // SUBC):
                     sub = slice(s * SUBC, (s + 1) * SUBC)
                     z = psum.tile([P, PACK, SUBC], F32, name="z%d_%d_%d" % (c, b, s), tag="z", bufs=4)
                     for t in range(PACK):
@@ -214,27 +240,57 @@ def tile_list_sleeper_crack_scores_kernel(
                             start=True,
                             stop=True,
                         )
-                    nc.scalar.activation(out=bent[:, sub, :], in_=z[:].rearrange("p t j -> p j t"), func=TANH)
-                dg = ring.tile([P, CH, PACK], BF16, name="dg%d_%d" % (c, b), tag="dg", bufs=3, align_bytes=64)
-                nc.vector.tensor_tensor(
-                    dg[:], bent[:], gain2_sb[:, b : b + 1, :].to_broadcast([P, CH, PACK]), MULT
-                )
-                moving.append(quantise(dg[:].rearrange("p c t -> p (c t)"), CH, "d%d_%d" % (c, b), ring, "d", 4))
+                    nc.scalar.activation(out=tile[:, sub, :], in_=z[:].rearrange("p t j -> p j t"), func=TANH)
 
-            staged = ring.tile([P, N // P, CH], F32, name="staged%d" % c, tag="staged")
-            for first, count in ((0, 2), (2, 1)):
-                acc = psum.tile([P, count, CH], F32, name="o%d_%d" % (c, first), tag="o", bufs=4)
-                for i in range(count):
-                    ncols = slice((first + i) * P, (first + i + 1) * P)
-                    for g in range(len(moving)):
+        def scores(c):
+            width = CHUNKS[c]
+            rounded = []
+            for b in range(mb):
+                dg = ring.tile([P, width, PACK], BF16, name="dg%d_%d" % (c, b), tag="dg", bufs=3, align_bytes=64)
+                nc.vector.tensor_tensor(
+                    dg[:], bent[(c, b)][:], gain2_rows[:, b, 0:width, :], MULT
+                )
+                rounded.append(dg)
+            moving = [xq[c]]
+            for b in range(mb):
+                moving.append(
+                    quantise(rounded[b][:].rearrange("p c t -> p (c t)"), width, "d%d_%d" % (c, b), ring, "d", 4)
+                )
+            per_bank = BANK // width
+            banks = []
+            for first in range(0, N // P, per_bank):
+                count = min(per_bank, N // P - first)
+                acc = psum.tile([P, count, width], F32, name="o%d_%d" % (c, first), tag="o", bufs=4)
+                banks.append((acc, first, count))
+            for g in range(len(moving)):
+                for acc, first, count in banks:
+                    for i in range(count):
+                        ncols = slice((first + i) * P, (first + i + 1) * P)
                         nc.tensor.matmul_mx(
                             out=acc[:, i, :],
                             lhsT=outw[g][0][:, ncols].bitcast(FP8X4),
                             lhsT_scale=outw[g][1][:, ncols],
                             rhs=moving[g][0][:].bitcast(FP8X4),
                             rhs_scale=moving[g][1][:],
-                            start=(g == 0),
-                            stop=(g == len(moving) - 1),
+                            start=(g == 0 and i == 0),
+                            stop=(g == len(moving) - 1 and i == count - 1),
                         )
+            sums[c] = banks
+
+        def store(c):
+            width = CHUNKS[c]
+            staged = ring.tile([P, N // P, width], F32, name="staged%d" % c, tag="staged", bufs=len(CHUNKS))
+            for acc, first, count in sums[c]:
                 nc.scalar.copy(out=staged[:, first : first + count, :], in_=acc[:])
-            nc.sync.dma_start(out=out_rows[:, :, cols], in_=staged[:])
+            nc.sync.dma_start(out=out_rows[:, :, starts[c] : starts[c] + width], in_=staged[:])
+
+        chunks = len(CHUNKS)
+        for step in range(chunks + 4):
+            if step < chunks:
+                differences(step)
+            if 0 <= step - 1 < chunks:
+                bend(step - 1)
+            if 0 <= step - 3 < chunks:
+                scores(step - 3)
+            if 0 <= step - 4 < chunks:
+                store(step - 4)

@@ -77,27 +77,37 @@ def tile_list_sleeper_crack_scores_kernel(
         nc.scalar.dma_start(out=gain_sb[:], in_=gain.rearrange("(p t) -> p t", t=PACK))
         nc.scalar.dma_start(out=gain2_sb[:], in_=gain2.rearrange("(b p t) -> p b t", p=P, t=PACK))
 
-        for a in range(ka):
-            words = keep.tile([P, T], I32, name="tab%d" % a, align_bytes=64)
+        def load_table(a):
+            words = keep.tile([P, T], I32, name="tab%d" % a, tag="tab%d" % a, align_bytes=64)
             nc.sync.dma_start(out=words[:], in_=tab_words[a].rearrange("p t i -> p (t i)").bitcast(I32))
-            raw = load_rows(w1[a * KP : (a + 1) * KP, :], "w1raw%d" % a)
-            if a == 0:
-                nc.sync.dma_start(out=wm_raw[:].bitcast(I32), in_=wm_words[0].bitcast(I32))
-                nc.sync.dma_start(out=wm_plane_raw[0:16, :].bitcast(I32), in_=wm_scales[0].bitcast(I32))
+            return words
+
+        def load_w1(a):
+            return load_rows(w1[a * KP : (a + 1) * KP, :], "w1raw%d" % a)
+
+        nc.sync.dma_start(out=wm_raw[:].bitcast(I32), in_=wm_words[0].bitcast(I32))
+        table = [load_table(0)]
+        nc.sync.dma_start(out=wm_plane_raw[0:16, :].bitcast(I32), in_=wm_scales[0].bitcast(I32))
+        table.append(load_table(1))
+        w1_raw = [load_w1(0)]
+        table.append(load_table(2))
+        w1_raw.extend([load_w1(1), load_w1(2)])
+
+        def pick_words(a):
             got = keep.tile([P, S], U32, name="picked%d" % a, align_bytes=64)
-            nc.vector.tensor_copy(got[:], words[:].bitcast(U32).indirect(list1[:]))
+            nc.vector.tensor_copy(got[:], table[a][:].bitcast(U32).indirect(list1[:]))
             picked.append(got)
-            if a == 0:
-                picked_plane = keep.tile([P, S], U8, name="picked_plane", align_bytes=64)
-                nc.vector.tensor_copy(picked_plane[:], tab_plane[:].indirect(list1[:]))
+
+        def quantise_w1(a):
             grouped = ring.tile([P, PACK, P, PACK], BF16, name="w1g%d" % a, tag="grouped", bufs=2, align_bytes=64)
             copy = nc.vector.tensor_copy if a == ka - 1 else nc.scalar.copy
             copy(
                 out=grouped[:].rearrange("p t m j -> p m j t"),
-                in_=raw[:].rearrange("p j (m t) -> p m j t", t=PACK),
+                in_=w1_raw[a][:].rearrange("p j (m t) -> p m j t", t=PACK),
             )
             w1q.append(quantise(grouped[:].rearrange("p t m j -> p (t m j)"), H, "w1q%d" % a, keep, "w1q%d" % a, 1))
 
+        pick_words(0)
         wm_codes = keep.tile([P, 2 * M], U8, name="wm_codes", align_bytes=64)
         nc.vector.tensor_copy(
             out=wm_codes[:].bitcast(U16).rearrange("p (b t q) -> p b t q", b=mb, t=PACK),
@@ -108,6 +118,12 @@ def tile_list_sleeper_crack_scores_kernel(
             out=wm_plane[:].rearrange("p (b t q) -> p b t q", b=mb, t=PACK),
             in_=wm_plane_raw[:].rearrange("p (b q t) -> p b t q", b=mb, t=PACK),
         )
+        pick_words(1)
+        picked_plane = keep.tile([P, S], U8, name="picked_plane", tag="tab1", align_bytes=64)
+        nc.vector.tensor_copy(picked_plane[:], tab_plane[:].indirect(list1[:]))
+        pick_words(2)
+        for a in range(ka):
+            quantise_w1(a)
         for q in range(1, 4):
             nc.gpsimd.dma_start(
                 out=wm_plane[32 * q : 32 * q + 4, :].bitcast(I32), in_=wm_plane[4 * q : 4 * q + 4, :].bitcast(I32)

from contextlib import ExitStack

import concourse.mybir as mybir

K, T, S, T2, PJ, H, M, N = 1536, 2048, 1024, 2048, 1024, 512, 1024, 384
FLOPS = 2 * (K * H * S + H * M * PJ + H * N * PJ + M * N * PJ)

F32 = mybir.dt.float32
BF16 = mybir.dt.bfloat16
I32 = mybir.dt.int32
U32 = mybir.dt.uint32
U16 = mybir.dt.uint16
U8 = mybir.dt.uint8
FP8X4 = mybir.dt.float8_e4m3fn_x4
FP4X4 = mybir.dt.float4_e2m1fn_x4
TANH = mybir.ActivationFunctionType.Tanh
COPY = mybir.ActivationFunctionType.Copy
MULT = mybir.AluOpType.mult
SUB = mybir.AluOpType.subtract

P = 128
PACK = 4
KP = P * PACK
BANK = 512
CHUNKS = (256, 256, 256, 128, 128)
SUBC = 128


def tile_list_sleeper_crack_scores_kernel(
    tc, tab_words, tab_scales, offs, w1, b1, gain, page0, wgs, offs2, offs3, offs4,
    wm_words, wm_scales, gain2, wd, wt, out,
):
    nc = tc.nc
    ka = K // KP
    mb = M // KP

    with ExitStack() as ctx:
        keep = ctx.enter_context(tc.tile_pool(name="keep", bufs=1))
        ring = ctx.enter_context(tc.tile_pool(name="ring", bufs=2))
        psum = ctx.enter_context(tc.psum_pool(name="psum", bufs=1))

        def load_list(src, name):
            tile = keep.tile([P, src.shape[1]], U16, name=name)
            nc.sync.dma_start(tile[:], src)
            return tile

        def load_rows(rows, name):
            raw = ring.tile([P, PACK, rows.shape[1]], F32, name=name, tag="raw", bufs=3)
            nc.sync.dma_start(out=raw[:], in_=rows.rearrange("(p j) w -> p j w", j=PACK))
            return raw

        def quantise(grouped, width, name, pool, tag, bufs):
            codes = pool.tile([P, width], U32, name=name + "_codes", tag=tag + "c", bufs=bufs, align_bytes=64)
            plane = pool.tile([P, width], U8, name=name + "_plane", tag=tag + "p", bufs=bufs, align_bytes=64)
            nc.vector.quantize_mx(out=codes[:].bitcast(FP8X4), scales=plane[:], in_=grouped)
            return codes, plane

        tab_plane = keep.tile([P, T], U8, name="tab_plane", align_bytes=64)
        nc.gpsimd.memset(tab_plane[:].bitcast(I32), 0)
        for q in range(4):
            nc.gpsimd.dma_start(
                out=tab_plane[32 * q : 32 * q + 4 * ka, :].bitcast(I32),
                in_=tab_scales[:, 4 * q : 4 * q + 4, :].bitcast(I32),
            )
        wm_plane_raw = keep.tile([P, M], U8, name="wm_plane_raw", align_bytes=64)
        nc.vector.memset(wm_plane_raw[:].bitcast(I32), 0)

        list1 = load_list(offs, "list1")
        wm_raw = keep.tile([P, 2 * M], U8, name="wm_raw", align_bytes=64)
        picked = []
        w1q = []
        b1_sb = keep.tile([P, PACK], F32, name="b1_sb")
        gain_sb = keep.tile([P, PACK], F32, name="gain_sb")

        gain2_sb = keep.tile([P, mb, PACK], F32, name="gain2_sb")
        nc.scalar.dma_start(out=b1_sb[:], in_=b1.rearrange("(p t) -> p t", t=PACK))
        nc.scalar.dma_start(out=gain_sb[:], in_=gain.rearrange("(p t) -> p t", t=PACK))
        nc.scalar.dma_start(out=gain2_sb[:], in_=gain2.rearrange("(b p t) -> p b t", p=P, t=PACK))

        def load_table(a):
            words = keep.tile([P, T], I32, name="tab%d" % a, tag="tab%d" % a, align_bytes=64)
            nc.sync.dma_start(out=words[:], in_=tab_words[a].rearrange("p t i -> p (t i)").bitcast(I32))
            return words

        def load_w1(a):
            return load_rows(w1[a * KP : (a + 1) * KP, :], "w1raw%d" % a)

        nc.sync.dma_start(out=wm_raw[:].bitcast(I32), in_=wm_words[0].bitcast(I32))
        table = [load_table(0)]
        nc.sync.dma_start(out=wm_plane_raw[0:16, :].bitcast(I32), in_=wm_scales[0].bitcast(I32))
        table.append(load_table(1))
        w1_raw = [load_w1(0)]
        table.append(load_table(2))
        w1_raw.extend([load_w1(1), load_w1(2)])

        def pick_words(a):
            got = keep.tile([P, S], U32, name="picked%d" % a, align_bytes=64)
            nc.vector.tensor_copy(got[:], table[a][:].bitcast(U32).indirect(list1[:]))
            picked.append(got)

        def quantise_w1(a):
            grouped = ring.tile([P, PACK, P, PACK], BF16, name="w1g%d" % a, tag="grouped", bufs=2, align_bytes=64)
            copy = nc.vector.tensor_copy if a == ka - 1 else nc.scalar.copy
            copy(
                out=grouped[:].rearrange("p t m j -> p m j t"),
                in_=w1_raw[a][:].rearrange("p j (m t) -> p m j t", t=PACK),
            )
            w1q.append(quantise(grouped[:].rearrange("p t m j -> p (t m j)"), H, "w1q%d" % a, keep, "w1q%d" % a, 1))

        pick_words(0)
        wm_codes = keep.tile([P, 2 * M], U8, name="wm_codes", align_bytes=64)
        nc.vector.tensor_copy(
            out=wm_codes[:].bitcast(U16).rearrange("p (b t q) -> p b t q", b=mb, t=PACK),
            in_=wm_raw[:].bitcast(U16).rearrange("p (b q t) -> p b t q", b=mb, t=PACK),
        )
        wm_plane = keep.tile([P, M], U8, name="wm_plane", align_bytes=64)
        nc.vector.tensor_copy(
            out=wm_plane[:].rearrange("p (b t q) -> p b t q", b=mb, t=PACK),
            in_=wm_plane_raw[:].rearrange("p (b q t) -> p b t q", b=mb, t=PACK),
        )
        pick_words(1)
        picked_plane = keep.tile([P, S], U8, name="picked_plane", tag="tab1", align_bytes=64)
        nc.vector.tensor_copy(picked_plane[:], tab_plane[:].indirect(list1[:]))
        pick_words(2)
        for a in range(ka):
            quantise_w1(a)
        for q in range(1, 4):
            nc.gpsimd.dma_start(
                out=wm_plane[32 * q : 32 * q + 4, :].bitcast(I32), in_=wm_plane[4 * q : 4 * q + 4, :].bitcast(I32)
            )

        page_rows = page0.rearrange("(p t) c -> p t c", t=PACK)
        wgs_rows = wgs.rearrange("(q t) j -> q t j", t=PACK)
        list4 = load_list(offs4, "list4")
        pages = [keep.tile([P, T2], F32, name="page%d" % t) for t in range(PACK)]
        wg = [keep.tile([P, S], F32, name="wg%d" % t) for t in range(PACK)]

        def load_wgs(t, cols):
            for q in (0, 2, 1, 3):
                nc.sync.dma_start(out=wg[t][32 * q : 32 * q + 32, cols], in_=wgs_rows[:, t, cols])

        nc.sync.dma_start(out=pages[0][:], in_=page_rows[:, 0, :])
        load_wgs(0, slice(0, BANK))
        list2 = load_list(offs2, "list2")
        load_wgs(0, slice(BANK, S))
        for t in range(1, PACK):
            nc.sync.dma_start(out=pages[t][:], in_=page_rows[:, t, :])
            load_wgs(t, slice(0, S))
            if t == 1:
                list3 = load_list(offs3, "list3")
                wd_raw = load_rows(wd, "wdraw")
            if t == 2:
                wt_raw = [load_rows(wt[b * KP : (b + 1) * KP, :], "wtraw%d" % b) for b in range(mb)]

        halves = S // BANK

        def stage1_pass(acc, t, half, a):
            codes, plane = w1q[a]
            cols = slice(half * BANK, (half + 1) * BANK)
            nc.tensor.matmul_mx(
                out=acc[:],
                lhsT=codes[:, t * P : (t + 1) * P].bitcast(FP8X4),
                lhsT_scale=plane[:, t * P : (t + 1) * P],
                rhs=picked[a][:, cols].bitcast(FP8X4),
                rhs_scale=picked_plane[4 * a : P, cols],
                start=(a == 0),
                stop=(a == ka - 1),
            )

        accs = {}
        for t in range(2):
            for half in range(halves):
                accs[(t, half)] = psum.tile([P, BANK], F32, name="h_acc%d%d" % (t, half), tag="z", bufs=4)
        for a in range(ka):
            for t in range(2):
                for half in range(halves):
                    stage1_pass(accs[(t, half)], t, half, a)

        before = []
        for t in range(PACK):
            old = keep.tile([P, PJ], F32, name="before%d" % t)
            nc.vector.tensor_copy(old[:], pages[t][:].indirect(list4[:]))
            before.append(old)
            feat = ring.tile([P, S], F32, name="feat%d" % t, tag="feat_or_diff")
            for half in range(halves):
                cols = slice(half * BANK, (half + 1) * BANK)
                nc.scalar.activation(out=wg[t][:, cols], in_=wg[t][:, cols], func=COPY, scale=gain_sb[:, t : t + 1])
                if t >= 2:
                    accs[(t, half)] = psum.tile([P, BANK], F32, name="h_acc%d%d" % (t, half), tag="z", bufs=4)
                    for a in range(ka):
                        stage1_pass(accs[(t, half)], t, half, a)
                nc.scalar.activation(
                    out=feat[:, cols], in_=accs[(t, half)][:], func=TANH, bias=b1_sb[:, t : t + 1]
                )
            pieces = halves if t == 0 else 1
            for piece in range(pieces):
                lo, hi = piece * S // pieces, (piece + 1) * S // pieces
                nc.vector.tensor_tensor(
                    pages[t][:].indirect(list2[:, lo // 16 : hi // 16]), feat[:, lo:hi], wg[t][:, lo:hi], MULT
                )

        gain2_rows = keep.tile([P, mb, max(CHUNKS), PACK], F32, name="gain2_rows")
        for b in range(mb):
            nc.scalar.copy(
                out=gain2_rows[:, b], in_=gain2_sb[:, b : b + 1, :].to_broadcast([P, max(CHUNKS), PACK])
            )

        def interleave(grouped, raw):
            nc.scalar.copy(
                out=grouped.rearrange("p (c i) t -> p c t i", i=4),
                in_=raw.rearrange("p t (c i) -> p c t i", i=4),
            )

        outw = []
        for name, raw in (("wd", wd_raw), ("wt0", wt_raw[0]), ("wt1", wt_raw[1])):
            grouped = ring.tile([P, N, PACK], BF16, name=name + "g", tag="grouped", bufs=2, align_bytes=64)
            interleave(grouped[:], raw[:])
            outw.append(quantise(grouped[:].rearrange("p n j -> p (n j)"), N, name, keep, name, 1))

        out_rows = out.rearrange("(i p) j -> p i j", p=P)
        starts = [sum(CHUNKS[:c]) for c in range(len(CHUNKS))]
        xq = {}
        bent = {}
        sums = {}

        def differences(c):
            width = CHUNKS[c]
            cols = slice(starts[c], starts[c] + width)
            diff = ring.tile([P, PACK, width], F32, name="diff%d" % c, tag="feat_or_diff")
            for t in range(PACK):
                nc.vector.tensor_tensor(
                    diff[:, t, :], pages[t][:].indirect(list3[:, cols.start // 16 : cols.stop // 16]),
                    before[t][:, cols], SUB,
                )
            xg = ring.tile([P, width, PACK], BF16, name="xg%d" % c, tag="xg", align_bytes=64)
            interleave(xg[:], diff[:])
            xq[c] = quantise(xg[:].rearrange("p c t -> p (c t)"), width, "x%d" % c, ring, "x", len(CHUNKS))

        def bend(c):
            width = CHUNKS[c]
            x_codes, x_plane = xq[c]
            for b in range(mb):
                tile = ring.tile([P, width, PACK], F32, name="bent%d_%d" % (c, b), tag="bent", bufs=6)
                bent[(c, b)] = tile
                for s in range(width // SUBC):
                    sub = slice(s * SUBC, (s + 1) * SUBC)
                    z = psum.tile([P, PACK, SUBC], F32, name="z%d_%d_%d" % (c, b, s), tag="z", bufs=4)
                    for t in range(PACK):
                        m0 = (b * PACK + t) * P
                        nc.tensor.matmul_mx(
                            out=z[:, t, :],
                            lhsT=wm_codes[:, 2 * m0 : 2 * (m0 + P)].bitcast(FP4X4),
                            lhsT_scale=wm_plane[:, m0 : m0 + P],
                            rhs=x_codes[:, sub].bitcast(FP8X4),
                            rhs_scale=x_plane[:, sub],
                            start=True,
                            stop=True,
                        )
                    nc.scalar.activation(out=tile[:, sub, :], in_=z[:].rearrange("p t j -> p j t"), func=TANH)

        def scores(c):
            width = CHUNKS[c]
            rounded = []
            for b in range(mb):
                dg = ring.tile([P, width, PACK], BF16, name="dg%d_%d" % (c, b), tag="dg", bufs=3, align_bytes=64)
                nc.vector.tensor_tensor(
                    dg[:], bent[(c, b)][:], gain2_rows[:, b, 0:width, :], MULT
                )
                rounded.append(dg)
            moving = [xq[c]]
            for b in range(mb):
                moving.append(
                    quantise(rounded[b][:].rearrange("p c t -> p (c t)"), width, "d%d_%d" % (c, b), ring, "d", 4)
                )
            per_bank = BANK // width
            banks = []
            for first in range(0, N // P, per_bank):
                count = min(per_bank, N // P - first)
                acc = psum.tile([P, count, width], F32, name="o%d_%d" % (c, first), tag="o", bufs=4)
                banks.append((acc, first, count))
            for g in range(len(moving)):
                for acc, first, count in banks:
                    for i in range(count):
                        ncols = slice((first + i) * P, (first + i + 1) * P)
                        nc.tensor.matmul_mx(
                            out=acc[:, i, :],
                            lhsT=outw[g][0][:, ncols].bitcast(FP8X4),
                            lhsT_scale=outw[g][1][:, ncols],
                            rhs=moving[g][0][:].bitcast(FP8X4),
                            rhs_scale=moving[g][1][:],
                            start=(g == 0 and i == 0),
                            stop=(g == len(moving) - 1 and i == count - 1),
                        )
            sums[c] = banks

        def store(c):
            width = CHUNKS[c]
            staged = ring.tile([P, N // P, width], F32, name="staged%d" % c, tag="staged", bufs=len(CHUNKS))
            for acc, first, count in sums[c]:
                nc.scalar.copy(out=staged[:, first : first + count, :], in_=acc[:])
            nc.sync.dma_start(out=out_rows[:, :, starts[c] : starts[c] + width], in_=staged[:])

        chunks = len(CHUNKS)
        for step in range(chunks + 4):
            if step < chunks:
                differences(step)
            if 0 <= step - 1 < chunks:
                bend(step - 1)
            if 0 <= step - 3 < chunks:
                scores(step - 3)
            if 0 <= step - 4 < chunks:
                store(step - 4)
